import numpy as np
import ml_dtypes


def mxq(x, axis, fmt="e4m3"):
    dtype, down = {"e4m3": (ml_dtypes.float8_e4m3fn, 7), "e5m2": (ml_dtypes.float8_e5m2, 14)}[fmt]
    v = np.moveaxis(np.asarray(x, np.float32).astype(ml_dtypes.bfloat16).astype(np.float64), axis, -1)
    blocks = v.reshape(v.shape[:-1] + (-1, 32))
    amax = np.abs(blocks).max(-1, keepdims=True)
    byte = np.maximum(np.where(amax > 0, np.frexp(amax)[1] - 1 + 127, 0) - down, 1)
    scale = np.exp2(byte - 127.0)
    codes = (blocks / scale).astype(np.float32).astype(dtype).astype(np.float64)
    return np.moveaxis((codes * scale).reshape(v.shape), -1, axis)


WIDE = False


def mx_kscale(k):
    if not WIDE:
        return np.ones(k)
    levels = np.array([24, -24, 12, -12, 0])
    if k % 512:
        return np.exp2(np.random.permutation(np.resize(levels, k // 32))).repeat(32)
    a = np.empty((k // 512, 16))
    for p in range(k // 512):
        a[p, :8] = np.random.permutation(np.resize(levels, 8))
        for g in range(8):
            far = levels[np.abs(levels - a[p, g]) >= 10]
            a[p, g + 8] = far[np.random.randint(len(far))]
    return np.exp2(a.ravel()).repeat(32)


def f64(x):
    return np.asarray(x).astype(np.float64)


def striped8(idx):
    return np.concatenate([v.reshape(-1, 16).T for v in idx]).astype(np.uint16)


def unstriped8(offs):
    return np.stack([offs[16 * g:16 * g + 16].T.reshape(-1) for g in range(8)]).astype(np.int64)


E2M1 = np.array([0.0, 0.5, 1.0, 1.5, 2.0, 3.0, 4.0, 6.0, -0.0, -0.5, -1.0, -1.5, -2.0, -3.0, -4.0, -6.0])


def pack_weight(w, fmt):
    k, n = w.shape
    w = f64(np.asarray(w, np.float32).astype(ml_dtypes.bfloat16)).reshape(k // 32, 32, n)
    amax = np.abs(w).max(1)
    if fmt == "e4m3":
        byte = np.frexp(amax)[1] - 1 + 127 - 7
    else:
        mant, ex = np.frexp(amax / 6.0)
        byte = np.where(mant > 0.5, ex, ex - 1) + 127
    byte = np.clip(np.where(amax > 0, byte, 1), 1, 254)
    scaled = (w * np.exp2(127.0 - byte)[:, None, :]).reshape(k, n).astype(np.float32)
    by_word = np.ascontiguousarray(scaled.reshape(k // 512, 128, 4, n).transpose(0, 1, 3, 2))
    if fmt == "e4m3":
        words = by_word.astype(ml_dtypes.float8_e4m3fn).view(np.uint8)
    else:
        c = by_word.astype(ml_dtypes.float4_e2m1fn).view(np.uint8) & 0xF
        words = (c[..., 0::2] | (c[..., 1::2] << 4)).reshape(k // 512, 128, 2 * n)
    return np.ascontiguousarray(words), np.ascontiguousarray(byte.astype(np.uint8).reshape(k // 512, 16, n))


def unpack_weight(words, scales, fmt):
    g, _, n = scales.shape
    words = np.ascontiguousarray(words).reshape(g, 128, n, -1)
    if fmt == "e4m3":
        vals = words.view(ml_dtypes.float8_e4m3fn).astype(np.float64)
    else:
        nib = np.empty((g, 128, n, 4), np.uint8)
        nib[..., 0::2] = words & 0xF
        nib[..., 1::2] = words >> 4
        vals = E2M1[nib]
    vals = vals * np.repeat(np.exp2(scales.astype(np.float64) - 127.0), 8, axis=1)[..., None]
    return vals.transpose(0, 1, 3, 2).reshape(g * 512, n)


K, L, N, T, J = 1024, 512, 512, 2048, 1024


def setup_inputs():
    n = np.random.standard_normal
    s = mx_kscale(K)[:, None]
    s2 = mx_kscale(L)[:, None]
    p_wx = pack_weight(n((L, N)) / np.sqrt(L) / s2, "e4m3")
    return {
        "xT": (n((K, T)) * s).astype(np.float32),
        "wgt": np.repeat(np.random.uniform(0.5, 2.0, (8, J)), 16, axis=0).astype(np.float32),
        "wt": (n((K, N)) / np.sqrt(K) / s).astype(np.float32),
        "c": (n((L, J)) * s2).astype(np.float32),
        "wx_words": p_wx[0],
        "wx_scales": p_wx[1],
        "wgo": np.repeat(np.random.uniform(0.5, 2.0, (8, J)), 16, axis=0).astype(np.float32),
        "offs": striped8(np.stack([np.random.permutation(T)[:J] for _ in range(8)])),
        "offs2": striped8(np.stack([np.random.permutation(T)[:J] for _ in range(8)])),
    }


def reference(xT, wgt, wt, c, wx_words, wx_scales, wgo, offs, offs2):
    idx = unstriped8(offs)
    idx2 = unstriped8(offs2)
    rows = np.arange(K)
    xg = f64(wgt)[rows // 4 % 128] * f64(xT)[rows[:, None], idx[rows % 512 // 64]]
    xT_ = mxq(xg, 0, "e4m3")
    wt_q_ = mxq(f64(wt), 0, "e4m3")
    wt_r_ = mxq(f64(wt) - wt_q_, 0, "e4m3")
    c_q_ = mxq(f64(c), 0, "e4m3")
    c_r_ = mxq(f64(c) - c_q_, 0, "e4m3")
    wx_ = unpack_weight(wx_words, wx_scales, "e4m3")
    y = wt_q_.T @ xT_ + wt_r_.T @ xT_ + wx_.T @ c_q_ + wx_.T @ c_r_
    out = np.zeros((N, T))
    rows = np.arange(N)
    out[rows[:, None], idx2[rows % 128 // 16]] = f64(wgo)[rows % 128] * (y)
    return out

@@ -1,0 +1,238 @@
+from contextlib import ExitStack
+
+import concourse.mybir as mybir
+from concourse.masks import make_identity
+
+K, L, N, T, J = 1024, 512, 512, 2048, 1024
+FLOPS = 2 * J * N * (2 * K + 2 * L) + 2 * 512 * (K * N + L * J)
+
+F32 = mybir.dt.float32
+BF16 = mybir.dt.bfloat16
+I32 = mybir.dt.int32
+U32 = mybir.dt.uint32
+U16 = mybir.dt.uint16
+U8 = mybir.dt.uint8
+FP8X4 = mybir.dt.float8_e4m3fn_x4
+MULT = mybir.AluOpType.mult
+SUBTRACT = mybir.AluOpType.subtract
+
+P = 128
+PACK = 4
+PASS = P * PACK
+HALF = 512
+UNIT = 256
+RUN = 2
+
+
+def by_rows(ap):
+    return ap.rearrange("p t (c i) -> p c t i", i=RUN)
+
+
+def by_words(ap):
+    return ap.rearrange("p (c i t) -> p c t i", i=RUN, t=PACK)
+
+
+def tile_list_tier_scat_kernel(
+    tc, xT, wgt, wt, c, wx_words, wx_scales, wgo, offs, offs2, out
+):
+    nc = tc.nc
+    with ExitStack() as ctx:
+        keep = ctx.enter_context(tc.tile_pool(name="keep", bufs=1))
+        ring = ctx.enter_context(tc.tile_pool(name="ring", bufs=2))
+        psum = ctx.enter_context(tc.psum_pool(name="psum", bufs=1))
+
+        def operand(name):
+            codes = keep.tile([P, HALF], U32, name=name + "_codes", align_bytes=64)
+            scales = keep.tile([P, HALF], U8, name=name + "_scales", align_bytes=64)
+            return codes, scales
+
+        def quantize(dst, col, src):
+            width = src.shape[1] // PACK
+            nc.vector.quantize_mx(
+                out=dst[0][:, col : col + width].bitcast(FP8X4),
+                scales=dst[1][:, col : col + width],
+                in_=src,
+            )
+
+        def matmul(acc, lhs, lcol, rhs, rcol, width, start, stop):
+            nc.tensor.matmul_mx(
+                out=acc,
+                lhsT=lhs[0][:, lcol : lcol + P].bitcast(FP8X4),
+                lhsT_scale=lhs[1][:, lcol : lcol + P],
+                rhs=rhs[0][:, rcol : rcol + width].bitcast(FP8X4),
+                rhs_scale=rhs[1][:, rcol : rcol + width],
+                start=start,
+                stop=stop,
+            )
+
+        picks = keep.tile([P, J // 16], U16, name="picks")
+        places = keep.tile([P, J // 16], U16, name="places")
+        wx = operand("wx")
+        nc.vector.memset(wx[1][:].bitcast(U32), 0)
+        for q in range(4):
+            nc.scalar.dma_start(
+                out=wx[1][32 * q : 32 * q + 4, :].bitcast(I32),
+                in_=wx_scales[0][4 * q : 4 * q + 4, :].bitcast(I32),
+            )
+
+        def load_rows(name, rows):
+            raw = keep.tile([P, PACK, rows.shape[1]], F32, name=name)
+            nc.sync.dma_start(out=raw[:], in_=rows.rearrange("(p t) w -> p t w", t=PACK))
+            return raw
+
+        x_planes = xT.rearrange("(a p t) w -> a t p w", p=P, t=PACK)
+        window = {}
+
+        def load_plane(a, t):
+            window[a, t] = keep.tile([P, T], F32, name="x%d%d" % (a, t))
+            nc.sync.dma_start(out=window[a, t][:], in_=x_planes[a][t])
+
+        wt0a = load_rows("wt0a", wt[0:PASS, 0:UNIT])
+        wt0b = load_rows("wt0b", wt[0:PASS, UNIT:N])
+        nc.sync.dma_start(picks[:], offs)
+        wgt0 = keep.tile([P, HALF], F32, name="wgt0", tag="late_picked")
+        nc.sync.dma_start(out=wgt0[:], in_=wgt[:, 0:HALF])
+        load_plane(0, 0)
+        wgt1 = keep.tile([P, HALF], F32, name="wgt1")
+        nc.sync.dma_start(out=wgt1[:], in_=wgt[:, HALF:J])
+        load_plane(0, 1)
+        wt1 = load_rows("wt1", wt[PASS:K, :])
+        load_plane(0, 2)
+        load_plane(0, 3)
+        c0 = load_rows("c0", c[:, 0:HALF])
+        nc.sync.dma_start(
+            out=wx[0][:].bitcast(I32), in_=wx_words[0].rearrange("p n i -> p (n i)").bitcast(I32)
+        )
+        load_plane(1, 0)
+        load_plane(1, 1)
+        c1 = load_rows("c1", c[:, HALF:J])
+        load_plane(1, 2)
+        load_plane(1, 3)
+        nc.sync.dma_start(places[:], offs2)
+        gain = keep.tile([P, J], F32, name="gain")
+        nc.sync.dma_start(out=gain[:], in_=wgo)
+        weight = [wgt0, wgt1]
+
+        eye = keep.tile([P, P], BF16, name="eye")
+        make_identity(nc, eye[:])
+        eye_words = ring.tile([P, PASS * PACK], BF16, name="eye_words", tag="x_words", align_bytes=64)
+        nc.vector.memset(eye_words[:], 0.0)
+        eye_view = eye_words[:].rearrange("p (j m i) -> p j m i", j=PACK, i=PACK)
+        for j in range(PACK):
+            nc.scalar.copy(out=eye_view[:, j, :, j], in_=eye[:])
+        ident = operand("ident")
+        quantize(ident, 0, eye_words[:])
+
+        turn = [0]
+
+        def first_tier(raw, rcol, q, col):
+            words = ring.tile([P, UNIT * PACK], BF16, name="first_words", bufs=3, align_bytes=64)
+            nc.scalar.copy(out=by_words(words[:]), in_=by_rows(raw[:, :, rcol : rcol + UNIT]))
+            quantize(q, col, words[:])
+            banks = []
+            for s in range(UNIT // P):
+                bank = psum.tile([P, PACK, P], F32, name="back", tag="bank%d" % (4 + turn[0] % 4))
+                turn[0] = turn[0] + 1
+                for t in range(PACK):
+                    matmul(bank[:, t, :], ident, t * P, q, col + s * P, P, True, True)
+                banks.append(bank)
+            return banks
+
+        def second_tier(raw, rcol, banks, r, col, words):
+            for s, bank in enumerate(banks):
+                nc.vector.tensor_tensor(
+                    out=by_words(words[:, s * PASS : (s + 1) * PASS]),
+                    in0=by_rows(raw[:, :, rcol + s * P : rcol + (s + 1) * P]),
+                    in1=by_rows(bank[:]),
+                    op=SUBTRACT,
+                )
+            quantize(r, col, words)
+
+        def both_tiers(raw, rcol, q, r, col):
+            banks = first_tier(raw, rcol, q, col)
+            words = ring.tile([P, UNIT * PACK], BF16, name="second_words", bufs=3, align_bytes=64)
+            second_tier(raw, rcol, banks, r, col, words[:])
+
+        def gather(dst, a, t, h):
+            nc.vector.tensor_tensor(
+                out=dst[:, t, :],
+                in0=window[a, t][:].indirect(picks[:, h * 32 : (h + 1) * 32]),
+                in1=weight[h][:],
+                op=MULT,
+            )
+
+        def quantize_picked(picked, words, dst):
+            for col in range(0, HALF, UNIT):
+                part = words[:, col * PACK : (col + UNIT) * PACK]
+                nc.scalar.copy(out=by_words(part), in_=by_rows(picked[:, :, col : col + UNIT]))
+                quantize(dst, col, part)
+
+        wq = [operand("wq0"), operand("wq1")]
+        wr = [operand("wr0"), operand("wr1")]
+        cq = [operand("cq0"), operand("cq1")]
+        cr = [operand("cr0"), operand("cr1")]
+        xg = {(a, h): operand("xg%d%d" % (a, h)) for a in range(2) for h in range(2)}
+
+        both_tiers(wt0a, 0, wq[0], wr[0], 0)
+        both_tiers(wt0b, 0, wq[0], wr[0], UNIT)
+        picked0 = [ring.tile([P, PACK, HALF], F32, name="picked0%d" % h, tag="picked") for h in range(2)]
+        for t in range(2):
+            for h in range(2):
+                gather(picked0[h], 0, t, h)
+        for col in range(0, N, UNIT):
+            both_tiers(wt1, col, wq[1], wr[1], col)
+        for t in range(2, PACK):
+            for h in range(2):
+                gather(picked0[h], 0, t, h)
+        for h in range(2):
+            words = ring.tile([P, HALF * PACK], BF16, name="x_words", tag="x_words", align_bytes=64)
+            quantize_picked(picked0[h], words[:], xg[0, h])
+        for col in range(0, HALF, UNIT):
+            both_tiers(c0, col, cq[0], cr[0], col)
+
+        def open_sums(h):
+            acc = [psum.tile([P, HALF], F32, name="acc", tag="bank%d" % (4 * h + t)) for t in range(4)]
+            for t in range(4):
+                matmul(acc[t][:], wq[0], t * P, xg[0, h], 0, HALF, True, False)
+                matmul(acc[t][:], wr[0], t * P, xg[0, h], 0, HALF, False, False)
+                matmul(acc[t][:], wx, t * P, cq[h], 0, HALF, False, False)
+                matmul(acc[t][:], wx, t * P, cr[h], 0, HALF, False, False)
+            return acc
+
+        pages = [keep.tile([P, T], F32, name="page%d" % t) for t in range(4)]
+
+        def close_sums(acc, h):
+            for t in range(4):
+                matmul(acc[t][:], wq[1], t * P, xg[1, h], 0, HALF, False, False)
+                matmul(acc[t][:], wr[1], t * P, xg[1, h], 0, HALF, False, True)
+                y = ring.tile([P, HALF], F32, name="y", bufs=4)
+                nc.scalar.copy(out=y[:], in_=acc[t][:])
+                nc.vector.tensor_tensor(
+                    out=pages[t][:].indirect(places[:, h * 32 : (h + 1) * 32]),
+                    in0=y[:],
+                    in1=gain[:, h * HALF : (h + 1) * HALF],
+                    op=MULT,
+                )
+                if h == 1:
+                    nc.sync.dma_start(out=out[t * P : (t + 1) * P, :], in_=pages[t][:])
+
+        acc0 = open_sums(0)
+        picked10 = ring.tile([P, PACK, HALF], F32, name="picked10", tag="picked")
+        for t in range(2):
+            gather(picked10, 1, t, 0)
+        c1_banks = first_tier(c1, 0, cq[1], 0) + first_tier(c1, UNIT, cq[1], UNIT)
+        for t in range(2, PACK):
+            gather(picked10, 1, t, 0)
+        words10 = keep.tile([P, HALF * PACK], BF16, name="words10", tag="late_words", align_bytes=64)
+        quantize_picked(picked10, words10[:], xg[1, 0])
+        picked11 = keep.tile([P, PACK, HALF], F32, name="picked11", tag="late_picked")
+        for t in range(PACK):
+            gather(picked11, 1, t, 1)
+        for t in range(4):
+            nc.vector.memset(pages[t][:], 0.0)
+        close_sums(acc0, 0)
+        c1_words = keep.tile([P, HALF * PACK], BF16, name="c1_words", tag="late_words", align_bytes=64)
+        second_tier(c1, 0, c1_banks, cr[1], 0, c1_words[:])
+        words11 = ring.tile([P, HALF * PACK], BF16, name="words11", tag="x_words", align_bytes=64)
+        quantize_picked(picked11, words11[:], xg[1, 1])
+        close_sums(open_sums(1), 1)

@@ -44,7 +44,7 @@ def tile_list_tier_scat_kernel(
         def operand(name):
             codes = keep.tile([P, HALF], U32, name=name + "_codes", align_bytes=64)
             scales = keep.tile([P, HALF], U8, name=name + "_scales", align_bytes=64)
-            return codes, scales
+            return codes[:], scales[:]
 
         def quantize(dst, col, src):
             width = src.shape[1] // PACK
@@ -69,11 +69,6 @@ def tile_list_tier_scat_kernel(
         places = keep.tile([P, J // 16], U16, name="places")
         wx = operand("wx")
         nc.vector.memset(wx[1][:].bitcast(U32), 0)
-        for q in range(4):
-            nc.scalar.dma_start(
-                out=wx[1][32 * q : 32 * q + 4, :].bitcast(I32),
-                in_=wx_scales[0][4 * q : 4 * q + 4, :].bitcast(I32),
-            )
 
         def load_rows(name, rows):
             raw = keep.tile([P, PACK, rows.shape[1]], F32, name=name)
@@ -84,61 +79,71 @@ def tile_list_tier_scat_kernel(
         window = {}
 
         def load_plane(a, t):
-            window[a, t] = keep.tile([P, T], F32, name="x%d%d" % (a, t))
+            window[a, t] = keep.tile([P, T], F32, name="x%d%d" % (a, t), tag="x%d%d" % (a, t))
             nc.sync.dma_start(out=window[a, t][:], in_=x_planes[a][t])
 
         wt0a = load_rows("wt0a", wt[0:PASS, 0:UNIT])
         wt0b = load_rows("wt0b", wt[0:PASS, UNIT:N])
+        wt1 = load_rows("wt1", wt[PASS:K, :])
+        c0 = load_rows("c0", c[:, 0:HALF])
+        c1 = load_rows("c1", c[:, HALF:J])
         nc.sync.dma_start(picks[:], offs)
-        wgt0 = keep.tile([P, HALF], F32, name="wgt0", tag="late_picked")
-        nc.sync.dma_start(out=wgt0[:], in_=wgt[:, 0:HALF])
+        late = keep.tile([P, PACK * HALF], F32, name="late", align_bytes=64)
+        wgt0 = late[:, 0:HALF]
+        nc.sync.dma_start(out=wgt0, in_=wgt[:, 0:HALF])
         load_plane(0, 0)
         wgt1 = keep.tile([P, HALF], F32, name="wgt1")
         nc.sync.dma_start(out=wgt1[:], in_=wgt[:, HALF:J])
         load_plane(0, 1)
-        wt1 = load_rows("wt1", wt[PASS:K, :])
         load_plane(0, 2)
         load_plane(0, 3)
-        c0 = load_rows("c0", c[:, 0:HALF])
         nc.sync.dma_start(
             out=wx[0][:].bitcast(I32), in_=wx_words[0].rearrange("p n i -> p (n i)").bitcast(I32)
         )
+        for q in range(4):
+            nc.sync.dma_start(
+                out=wx[1][32 * q : 32 * q + 4, :].bitcast(I32),
+                in_=wx_scales[0][4 * q : 4 * q + 4, :].bitcast(I32),
+            )
         load_plane(1, 0)
         load_plane(1, 1)
-        c1 = load_rows("c1", c[:, HALF:J])
         load_plane(1, 2)
         load_plane(1, 3)
         nc.sync.dma_start(places[:], offs2)
         gain = keep.tile([P, J], F32, name="gain")
         nc.sync.dma_start(out=gain[:], in_=wgo)
-        weight = [wgt0, wgt1]
+        weight = [wgt0, wgt1[:]]
 
         eye = keep.tile([P, P], BF16, name="eye")
         make_identity(nc, eye[:])
-        eye_words = ring.tile([P, PASS * PACK], BF16, name="eye_words", tag="x_words", align_bytes=64)
+        eye_words = ring.tile([P, PASS * PACK], BF16, name="eye_words", tag="first_words", align_bytes=64)
         nc.vector.memset(eye_words[:], 0.0)
         eye_view = eye_words[:].rearrange("p (j m i) -> p j m i", j=PACK, i=PACK)
         for j in range(PACK):
-            nc.scalar.copy(out=eye_view[:, j, :, j], in_=eye[:])
+            nc.vector.tensor_copy(out=eye_view[:, j, :, j], in_=eye[:])
         ident = operand("ident")
         quantize(ident, 0, eye_words[:])
 
+        eye32 = keep.tile([P, P], F32, name="eye32")
+        make_identity(nc, eye32[:])
         turn = [0]
 
-        def first_tier(raw, rcol, q, col):
-            words = ring.tile([P, UNIT * PACK], BF16, name="first_words", bufs=3, align_bytes=64)
+        def first_tier(raw, rcol, q, col, tag="first_words"):
+            words = ring.tile([P, UNIT * PACK], BF16, name="first_words", tag=tag, align_bytes=64)
             nc.scalar.copy(out=by_words(words[:]), in_=by_rows(raw[:, :, rcol : rcol + UNIT]))
             quantize(q, col, words[:])
+
+        def bring_back(q, col):
             banks = []
             for s in range(UNIT // P):
-                bank = psum.tile([P, PACK, P], F32, name="back", tag="bank%d" % (4 + turn[0] % 4))
+                bank = psum.tile([P, PACK, P], F32, name="back", tag="bank%d" % (4 + turn[0] % 2))
                 turn[0] = turn[0] + 1
                 for t in range(PACK):
                     matmul(bank[:, t, :], ident, t * P, q, col + s * P, P, True, True)
                 banks.append(bank)
             return banks
 
-        def second_tier(raw, rcol, banks, r, col, words):
+        def leftover(raw, rcol, banks, words):
             for s, bank in enumerate(banks):
                 nc.vector.tensor_tensor(
                     out=by_words(words[:, s * PASS : (s + 1) * PASS]),
@@ -146,18 +151,53 @@ def tile_list_tier_scat_kernel(
                     in1=by_rows(bank[:]),
                     op=SUBTRACT,
                 )
-            quantize(r, col, words)
 
-        def both_tiers(raw, rcol, q, r, col):
-            banks = first_tier(raw, rcol, q, col)
-            words = ring.tile([P, UNIT * PACK], BF16, name="second_words", bufs=3, align_bytes=64)
-            second_tier(raw, rcol, banks, r, col, words[:])
+        def both_tiers(raw, rcol, q, r, col, tag):
+            first_tier(raw, rcol, q, col, tag)
+            banks = bring_back(q, col)
+            words = ring.tile([P, UNIT * PACK], BF16, name="second_words", align_bytes=64)
+            leftover(raw, rcol, banks, words[:])
+            quantize(r, col, words[:])
+
+        def leftover_on_tensor(raw, rcol, banks, words):
+            back = psum.tile([P, UNIT // P, 2, P], F32, name="back_words", tag="bank7")
+            for s, bank in enumerate(banks):
+                minus = ring.tile([P, PACK, P], F32, name="minus")
+                nc.scalar.mul(minus[:], bank[:], -1.0)
+                total = psum.tile([P, PACK, P], F32, name="total", tag=["bank6", "bank3"][s])
+                for t in range(PACK):
+                    nc.tensor.matmul(
+                        total[:, t, :], minus[:, t, :], eye32[:], is_transpose=True, start=True, stop=False
+                    )
+                    nc.tensor.matmul(
+                        total[:, t, :], raw[:, t, rcol + s * P : rcol + (s + 1) * P], eye32[:],
+                        is_transpose=True, start=False, stop=True,
+                    )
+                turned = ring.tile([P, PASS], BF16, name="turned")
+                nc.scalar.copy(
+                    out=turned[:].rearrange("n (u p e) -> n u p e", u=2, e=2),
+                    in_=total[:].rearrange("n (u e) p -> n u p e", u=2),
+                )
+                pairs = turned[:].bitcast(F32)
+                for u in range(2):
+                    nc.tensor.transpose(back[:, s, u, :], pairs[:, u * P : (u + 1) * P], eye32[:])
+            nc.scalar.copy(
+                out=words.bitcast(F32).rearrange("p (s n u) -> p s n u", s=UNIT // P, u=2),
+                in_=back[:].rearrange("p s u n -> p s n u"),
+            )
+
+        def second_tier_wide(raw, q, r, leftover):
+            words = ring.tile([P, HALF * PACK], BF16, name="wide_words", align_bytes=64)
+            for col in range(0, HALF, UNIT):
+                banks = bring_back(q, col)
+                leftover(raw, col, banks, words[:, col * PACK : (col + UNIT) * PACK])
+            quantize(r, 0, words[:])
 
         def gather(dst, a, t, h):
             nc.vector.tensor_tensor(
                 out=dst[:, t, :],
                 in0=window[a, t][:].indirect(picks[:, h * 32 : (h + 1) * 32]),
-                in1=weight[h][:],
+                in1=weight[h],
                 op=MULT,
             )
 
@@ -167,28 +207,33 @@ def tile_list_tier_scat_kernel(
                 nc.scalar.copy(out=by_words(part), in_=by_rows(picked[:, :, col : col + UNIT]))
                 quantize(dst, col, part)
 
-        wq = [operand("wq0"), operand("wq1")]
+        wq0_codes = keep.tile([P, HALF], U32, name="wq0_codes", align_bytes=64)
+        wq1_codes = keep.tile([P, HALF], U32, name="wq1_codes", align_bytes=64)
+        wq = [(wq0_codes[:], ident[1][4:P, :]), (wq1_codes[:], ident[1][8:P, :])]
         wr = [operand("wr0"), operand("wr1")]
         cq = [operand("cq0"), operand("cq1")]
         cr = [operand("cr0"), operand("cr1")]
         xg = {(a, h): operand("xg%d%d" % (a, h)) for a in range(2) for h in range(2)}
 
-        both_tiers(wt0a, 0, wq[0], wr[0], 0)
-        both_tiers(wt0b, 0, wq[0], wr[0], UNIT)
-        picked0 = [ring.tile([P, PACK, HALF], F32, name="picked0%d" % h, tag="picked") for h in range(2)]
-        for t in range(2):
-            for h in range(2):
-                gather(picked0[h], 0, t, h)
-        for col in range(0, N, UNIT):
-            both_tiers(wt1, col, wq[1], wr[1], col)
-        for t in range(2, PACK):
+        both_tiers(wt0a, 0, wq[0], wr[0], 0, "first_words")
+        both_tiers(wt0b, 0, wq[0], wr[0], UNIT, "first_words")
+        for col in range(0, HALF, UNIT):
+            first_tier(wt1, col, wq[1], col)
+        second_tier_wide(wt1, wq[1], wr[1], leftover)
+        for raw, q in ((c0, cq[0]), (c1, cq[1])):
+            for col in range(0, HALF, UNIT):
+                first_tier(raw, col, q, col)
+        second_tier_wide(c0, cq[0], cr[0], leftover_on_tensor)
+        second_tier_wide(c1, cq[1], cr[1], leftover_on_tensor)
+        picked0 = [
+            ring.tile([P, PACK, HALF], F32, name="picked0%d" % h, tag="picked", align_bytes=64) for h in range(2)
+        ]
+        for t in range(PACK):
             for h in range(2):
                 gather(picked0[h], 0, t, h)
         for h in range(2):
-            words = ring.tile([P, HALF * PACK], BF16, name="x_words", tag="x_words", align_bytes=64)
+            words = ring.tile([P, HALF * PACK], BF16, name="x_words", tag="wide_words", align_bytes=64)
             quantize_picked(picked0[h], words[:], xg[0, h])
-        for col in range(0, HALF, UNIT):
-            both_tiers(c0, col, cq[0], cr[0], col)
 
         def open_sums(h):
             acc = [psum.tile([P, HALF], F32, name="acc", tag="bank%d" % (4 * h + t)) for t in range(4)]
@@ -199,13 +244,16 @@ def tile_list_tier_scat_kernel(
                 matmul(acc[t][:], wx, t * P, cr[h], 0, HALF, False, False)
             return acc
 
-        pages = [keep.tile([P, T], F32, name="page%d" % t) for t in range(4)]
+        pages = {}
 
-        def close_sums(acc, h):
-            for t in range(4):
+        def close_sums(acc, h, tiles):
+            for t in tiles:
                 matmul(acc[t][:], wq[1], t * P, xg[1, h], 0, HALF, False, False)
                 matmul(acc[t][:], wr[1], t * P, xg[1, h], 0, HALF, False, True)
-                y = ring.tile([P, HALF], F32, name="y", bufs=4)
+                if h == 0 and t < 2:
+                    y = keep.tile([P, HALF], F32, name="y", tag="slot%d" % (t + 2))
+                else:
+                    y = ring.tile([P, HALF], F32, name="y", bufs=4)
                 nc.scalar.copy(out=y[:], in_=acc[t][:])
                 nc.vector.tensor_tensor(
                     out=pages[t][:].indirect(places[:, h * 32 : (h + 1) * 32]),
@@ -217,22 +265,24 @@ def tile_list_tier_scat_kernel(
                     nc.sync.dma_start(out=out[t * P : (t + 1) * P, :], in_=pages[t][:])
 
         acc0 = open_sums(0)
-        picked10 = ring.tile([P, PACK, HALF], F32, name="picked10", tag="picked")
+        picked10 = keep.tile([P, PACK, HALF], F32, name="picked10")
         for t in range(2):
             gather(picked10, 1, t, 0)
-        c1_banks = first_tier(c1, 0, cq[1], 0) + first_tier(c1, UNIT, cq[1], UNIT)
         for t in range(2, PACK):
             gather(picked10, 1, t, 0)
-        words10 = keep.tile([P, HALF * PACK], BF16, name="words10", tag="late_words", align_bytes=64)
-        quantize_picked(picked10, words10[:], xg[1, 0])
-        picked11 = keep.tile([P, PACK, HALF], F32, name="picked11", tag="late_picked")
+        quantize_picked(picked10, late[:, 2 * HALF : PACK * HALF].bitcast(BF16), xg[1, 0])
+        picked11 = late[:].rearrange("p (t w) -> p t w", t=PACK)
         for t in range(PACK):
             gather(picked11, 1, t, 1)
-        for t in range(4):
-            nc.vector.memset(pages[t][:], 0.0)
-        close_sums(acc0, 0)
-        c1_words = keep.tile([P, HALF * PACK], BF16, name="c1_words", tag="late_words", align_bytes=64)
-        second_tier(c1, 0, c1_banks, cr[1], 0, c1_words[:])
-        words11 = ring.tile([P, HALF * PACK], BF16, name="words11", tag="x_words", align_bytes=64)
+        pages[0] = keep.tile([P, T], F32, name="page0", tag="x00")
+        for col in range(0, T, HALF):
+            nc.gpsimd.memset(pages[0][:, col : col + HALF].bitcast(U32), 0)
+        for t in range(3):
+            close_sums(acc0, 0, [t])
+            pages[t + 1] = keep.tile([P, T], F32, name="page", tag=["x13", "slot2", "slot3"][t])
+            nc.gpsimd.memset(pages[t + 1][:].bitcast(U32), 0)
+        words11 = keep.tile([P, HALF * PACK], BF16, name="words11", align_bytes=64)
         quantize_picked(picked11, words11[:], xg[1, 1])
-        close_sums(open_sums(1), 1)
+        close_sums(acc0, 0, [3])
+        acc1 = open_sums(1)
+        close_sums(acc1, 1, range(4))

from contextlib import ExitStack

import concourse.mybir as mybir
from concourse.masks import make_identity

K, L, N, T, J = 1024, 512, 512, 2048, 1024
FLOPS = 2 * J * N * (2 * K + 2 * L) + 2 * 512 * (K * N + L * J)

F32 = mybir.dt.float32
BF16 = mybir.dt.bfloat16
I32 = mybir.dt.int32
U32 = mybir.dt.uint32
U16 = mybir.dt.uint16
U8 = mybir.dt.uint8
FP8X4 = mybir.dt.float8_e4m3fn_x4
MULT = mybir.AluOpType.mult
SUBTRACT = mybir.AluOpType.subtract

P = 128
PACK = 4
PASS = P * PACK
HALF = 512
UNIT = 256
RUN = 2


def by_rows(ap):
    return ap.rearrange("p t (c i) -> p c t i", i=RUN)


def by_words(ap):
    return ap.rearrange("p (c i t) -> p c t i", i=RUN, t=PACK)


def tile_list_tier_scat_kernel(
    tc, xT, wgt, wt, c, wx_words, wx_scales, wgo, offs, offs2, out
):
    nc = tc.nc
    with ExitStack() as ctx:
        keep = ctx.enter_context(tc.tile_pool(name="keep", bufs=1))
        ring = ctx.enter_context(tc.tile_pool(name="ring", bufs=2))
        psum = ctx.enter_context(tc.psum_pool(name="psum", bufs=1))

        def operand(name):
            codes = keep.tile([P, HALF], U32, name=name + "_codes", align_bytes=64)
            scales = keep.tile([P, HALF], U8, name=name + "_scales", align_bytes=64)
            return codes[:], scales[:]

        def quantize(dst, col, src):
            width = src.shape[1] // PACK
            nc.vector.quantize_mx(
                out=dst[0][:, col : col + width].bitcast(FP8X4),
                scales=dst[1][:, col : col + width],
                in_=src,
            )

        def matmul(acc, lhs, lcol, rhs, rcol, width, start, stop):
            nc.tensor.matmul_mx(
                out=acc,
                lhsT=lhs[0][:, lcol : lcol + P].bitcast(FP8X4),
                lhsT_scale=lhs[1][:, lcol : lcol + P],
                rhs=rhs[0][:, rcol : rcol + width].bitcast(FP8X4),
                rhs_scale=rhs[1][:, rcol : rcol + width],
                start=start,
                stop=stop,
            )

        picks = keep.tile([P, J // 16], U16, name="picks")
        places = keep.tile([P, J // 16], U16, name="places")
        wx = operand("wx")
        nc.vector.memset(wx[1][:].bitcast(U32), 0)

        def load_rows(name, rows):
            raw = keep.tile([P, PACK, rows.shape[1]], F32, name=name)
            nc.sync.dma_start(out=raw[:], in_=rows.rearrange("(p t) w -> p t w", t=PACK))
            return raw

        x_planes = xT.rearrange("(a p t) w -> a t p w", p=P, t=PACK)
        window = {}

        def load_plane(a, t):
            window[a, t] = keep.tile([P, T], F32, name="x%d%d" % (a, t), tag="x%d%d" % (a, t))
            nc.sync.dma_start(out=window[a, t][:], in_=x_planes[a][t])

        wt0a = load_rows("wt0a", wt[0:PASS, 0:UNIT])
        wt0b = load_rows("wt0b", wt[0:PASS, UNIT:N])
        wt1 = load_rows("wt1", wt[PASS:K, :])
        c0 = load_rows("c0", c[:, 0:HALF])
        c1 = load_rows("c1", c[:, HALF:J])
        nc.sync.dma_start(picks[:], offs)
        late = keep.tile([P, PACK * HALF], F32, name="late", align_bytes=64)
        wgt0 = late[:, 0:HALF]
        nc.sync.dma_start(out=wgt0, in_=wgt[:, 0:HALF])
        load_plane(0, 0)
        wgt1 = keep.tile([P, HALF], F32, name="wgt1")
        nc.sync.dma_start(out=wgt1[:], in_=wgt[:, HALF:J])
        load_plane(0, 1)
        load_plane(0, 2)
        load_plane(0, 3)
        nc.sync.dma_start(
            out=wx[0][:].bitcast(I32), in_=wx_words[0].rearrange("p n i -> p (n i)").bitcast(I32)
        )
        for q in range(4):
            nc.sync.dma_start(
                out=wx[1][32 * q : 32 * q + 4, :].bitcast(I32),
                in_=wx_scales[0][4 * q : 4 * q + 4, :].bitcast(I32),
            )
        load_plane(1, 0)
        load_plane(1, 1)
        load_plane(1, 2)
        load_plane(1, 3)
        nc.sync.dma_start(places[:], offs2)
        gain = keep.tile([P, J], F32, name="gain")
        nc.sync.dma_start(out=gain[:], in_=wgo)
        weight = [wgt0, wgt1[:]]

        eye = keep.tile([P, P], BF16, name="eye")
        make_identity(nc, eye[:])
        eye_words = ring.tile([P, PASS * PACK], BF16, name="eye_words", tag="first_words", align_bytes=64)
        nc.vector.memset(eye_words[:], 0.0)
        eye_view = eye_words[:].rearrange("p (j m i) -> p j m i", j=PACK, i=PACK)
        for j in range(PACK):
            nc.vector.tensor_copy(out=eye_view[:, j, :, j], in_=eye[:])
        ident = operand("ident")
        quantize(ident, 0, eye_words[:])

        eye32 = keep.tile([P, P], F32, name="eye32")
        make_identity(nc, eye32[:])
        turn = [0]

        def first_tier(raw, rcol, q, col, tag="first_words"):
            words = ring.tile([P, UNIT * PACK], BF16, name="first_words", tag=tag, align_bytes=64)
            nc.scalar.copy(out=by_words(words[:]), in_=by_rows(raw[:, :, rcol : rcol + UNIT]))
            quantize(q, col, words[:])

        def bring_back(q, col):
            banks = []
            for s in range(UNIT // P):
                bank = psum.tile([P, PACK, P], F32, name="back", tag="bank%d" % (4 + turn[0] % 2))
                turn[0] = turn[0] + 1
                for t in range(PACK):
                    matmul(bank[:, t, :], ident, t * P, q, col + s * P, P, True, True)
                banks.append(bank)
            return banks

        def leftover(raw, rcol, banks, words):
            for s, bank in enumerate(banks):
                nc.vector.tensor_tensor(
                    out=by_words(words[:, s * PASS : (s + 1) * PASS]),
                    in0=by_rows(raw[:, :, rcol + s * P : rcol + (s + 1) * P]),
                    in1=by_rows(bank[:]),
                    op=SUBTRACT,
                )

        def both_tiers(raw, rcol, q, r, col, tag):
            first_tier(raw, rcol, q, col, tag)
            banks = bring_back(q, col)
            words = ring.tile([P, UNIT * PACK], BF16, name="second_words", align_bytes=64)
            leftover(raw, rcol, banks, words[:])
            quantize(r, col, words[:])

        def leftover_on_tensor(raw, rcol, banks, words):
            back = psum.tile([P, UNIT // P, 2, P], F32, name="back_words", tag="bank7")
            for s, bank in enumerate(banks):
                minus = ring.tile([P, PACK, P], F32, name="minus")
                nc.scalar.mul(minus[:], bank[:], -1.0)
                total = psum.tile([P, PACK, P], F32, name="total", tag=["bank6", "bank3"][s])
                for t in range(PACK):
                    nc.tensor.matmul(
                        total[:, t, :], minus[:, t, :], eye32[:], is_transpose=True, start=True, stop=False
                    )
                    nc.tensor.matmul(
                        total[:, t, :], raw[:, t, rcol + s * P : rcol + (s + 1) * P], eye32[:],
                        is_transpose=True, start=False, stop=True,
                    )
                turned = ring.tile([P, PASS], BF16, name="turned")
                nc.scalar.copy(
                    out=turned[:].rearrange("n (u p e) -> n u p e", u=2, e=2),
                    in_=total[:].rearrange("n (u e) p -> n u p e", u=2),
                )
                pairs = turned[:].bitcast(F32)
                for u in range(2):
                    nc.tensor.transpose(back[:, s, u, :], pairs[:, u * P : (u + 1) * P], eye32[:])
            nc.scalar.copy(
                out=words.bitcast(F32).rearrange("p (s n u) -> p s n u", s=UNIT // P, u=2),
                in_=back[:].rearrange("p s u n -> p s n u"),
            )

        def second_tier_wide(raw, q, r, leftover):
            words = ring.tile([P, HALF * PACK], BF16, name="wide_words", align_bytes=64)
            for col in range(0, HALF, UNIT):
                banks = bring_back(q, col)
                leftover(raw, col, banks, words[:, col * PACK : (col + UNIT) * PACK])
            quantize(r, 0, words[:])

        def gather(dst, a, t, h):
            nc.vector.tensor_tensor(
                out=dst[:, t, :],
                in0=window[a, t][:].indirect(picks[:, h * 32 : (h + 1) * 32]),
                in1=weight[h],
                op=MULT,
            )

        def quantize_picked(picked, words, dst):
            for col in range(0, HALF, UNIT):
                part = words[:, col * PACK : (col + UNIT) * PACK]
                nc.scalar.copy(out=by_words(part), in_=by_rows(picked[:, :, col : col + UNIT]))
                quantize(dst, col, part)

        wq0_codes = keep.tile([P, HALF], U32, name="wq0_codes", align_bytes=64)
        wq1_codes = keep.tile([P, HALF], U32, name="wq1_codes", align_bytes=64)
        wq = [(wq0_codes[:], ident[1][4:P, :]), (wq1_codes[:], ident[1][8:P, :])]
        wr = [operand("wr0"), operand("wr1")]
        cq = [operand("cq0"), operand("cq1")]
        cr = [operand("cr0"), operand("cr1")]
        xg = {(a, h): operand("xg%d%d" % (a, h)) for a in range(2) for h in range(2)}

        both_tiers(wt0a, 0, wq[0], wr[0], 0, "first_words")
        both_tiers(wt0b, 0, wq[0], wr[0], UNIT, "first_words")
        for col in range(0, HALF, UNIT):
            first_tier(wt1, col, wq[1], col)
        second_tier_wide(wt1, wq[1], wr[1], leftover)
        for raw, q in ((c0, cq[0]), (c1, cq[1])):
            for col in range(0, HALF, UNIT):
                first_tier(raw, col, q, col)
        second_tier_wide(c0, cq[0], cr[0], leftover_on_tensor)
        second_tier_wide(c1, cq[1], cr[1], leftover_on_tensor)
        picked0 = [
            ring.tile([P, PACK, HALF], F32, name="picked0%d" % h, tag="picked", align_bytes=64) for h in range(2)
        ]
        for t in range(PACK):
            for h in range(2):
                gather(picked0[h], 0, t, h)
        for h in range(2):
            words = ring.tile([P, HALF * PACK], BF16, name="x_words", tag="wide_words", align_bytes=64)
            quantize_picked(picked0[h], words[:], xg[0, h])

        def open_sums(h):
            acc = [psum.tile([P, HALF], F32, name="acc", tag="bank%d" % (4 * h + t)) for t in range(4)]
            for t in range(4):
                matmul(acc[t][:], wq[0], t * P, xg[0, h], 0, HALF, True, False)
                matmul(acc[t][:], wr[0], t * P, xg[0, h], 0, HALF, False, False)
                matmul(acc[t][:], wx, t * P, cq[h], 0, HALF, False, False)
                matmul(acc[t][:], wx, t * P, cr[h], 0, HALF, False, False)
            return acc

        pages = {}

        def close_sums(acc, h, tiles):
            for t in tiles:
                matmul(acc[t][:], wq[1], t * P, xg[1, h], 0, HALF, False, False)
                matmul(acc[t][:], wr[1], t * P, xg[1, h], 0, HALF, False, True)
                if h == 0 and t < 2:
                    y = keep.tile([P, HALF], F32, name="y", tag="slot%d" % (t + 2))
                else:
                    y = ring.tile([P, HALF], F32, name="y", bufs=4)
                nc.scalar.copy(out=y[:], in_=acc[t][:])
                nc.vector.tensor_tensor(
                    out=pages[t][:].indirect(places[:, h * 32 : (h + 1) * 32]),
                    in0=y[:],
                    in1=gain[:, h * HALF : (h + 1) * HALF],
                    op=MULT,
                )
                if h == 1:
                    nc.sync.dma_start(out=out[t * P : (t + 1) * P, :], in_=pages[t][:])

        acc0 = open_sums(0)
        picked10 = keep.tile([P, PACK, HALF], F32, name="picked10")
        for t in range(2):
            gather(picked10, 1, t, 0)
        for t in range(2, PACK):
            gather(picked10, 1, t, 0)
        quantize_picked(picked10, late[:, 2 * HALF : PACK * HALF].bitcast(BF16), xg[1, 0])
        picked11 = late[:].rearrange("p (t w) -> p t w", t=PACK)
        for t in range(PACK):
            gather(picked11, 1, t, 1)
        pages[0] = keep.tile([P, T], F32, name="page0", tag="x00")
        for col in range(0, T, HALF):
            nc.gpsimd.memset(pages[0][:, col : col + HALF].bitcast(U32), 0)
        for t in range(3):
            close_sums(acc0, 0, [t])
            pages[t + 1] = keep.tile([P, T], F32, name="page", tag=["x13", "slot2", "slot3"][t])
            nc.gpsimd.memset(pages[t + 1][:].bitcast(U32), 0)
        words11 = keep.tile([P, HALF * PACK], BF16, name="words11", align_bytes=64)
        quantize_picked(picked11, words11[:], xg[1, 1])
        close_sums(acc0, 0, [3])
        acc1 = open_sums(1)
        close_sums(acc1, 1, range(4))
